import numpy as np
import ml_dtypes


def mxq(x, axis, fmt="e4m3"):
    dtype, down = {"e4m3": (ml_dtypes.float8_e4m3fn, 7), "e5m2": (ml_dtypes.float8_e5m2, 14)}[fmt]
    v = np.moveaxis(np.asarray(x, np.float32).astype(ml_dtypes.bfloat16).astype(np.float64), axis, -1)
    blocks = v.reshape(v.shape[:-1] + (-1, 32))
    amax = np.abs(blocks).max(-1, keepdims=True)
    byte = np.maximum(np.where(amax > 0, np.frexp(amax)[1] - 1 + 127, 0) - down, 1)
    scale = np.exp2(byte - 127.0)
    codes = (blocks / scale).astype(np.float32).astype(dtype).astype(np.float64)
    return np.moveaxis((codes * scale).reshape(v.shape), -1, axis)


WIDE = False


def mx_kscale(k):
    if not WIDE:
        return np.ones(k)
    levels = np.array([10, -10, 5, -5, 0])
    if k % 512:
        return np.exp2(np.random.permutation(np.resize(levels, k // 32))).repeat(32)
    a = np.empty((k // 512, 16))
    for p in range(k // 512):
        a[p, :8] = np.random.permutation(np.resize(levels, 8))
        for g in range(8):
            far = levels[np.abs(levels - a[p, g]) >= 10]
            a[p, g + 8] = far[np.random.randint(len(far))]
    return np.exp2(a.ravel()).repeat(32)


def f64(x):
    return np.asarray(x).astype(np.float64)


def striped(idx):
    return np.tile(idx.reshape(-1, 16).T, (8, 1)).astype(np.uint16)


def unstriped(offs):
    return offs[:16].T.reshape(-1).astype(np.int64)


def pack_weight(w):
    k, n = w.shape
    w = f64(np.asarray(w, np.float32).astype(ml_dtypes.bfloat16)).reshape(k // 32, 32, n)
    amax = np.abs(w).max(1)
    byte = np.clip(np.where(amax > 0, np.frexp(amax)[1] - 1 + 127 - 7, 1), 1, 254)
    scaled = (w * np.exp2(127.0 - byte)[:, None, :]).reshape(k, n).astype(np.float32)
    words = np.ascontiguousarray(scaled.reshape(k // 512, 128, 4, n).transpose(0, 1, 3, 2)).astype(ml_dtypes.float8_e4m3fn).view(np.uint8)
    return words, np.ascontiguousarray(byte.astype(np.uint8).reshape(k // 512, 16, n))


def unpack_weight(words, scales):
    g, p, n, _ = words.shape
    vals = np.ascontiguousarray(words).view(ml_dtypes.float8_e4m3fn).astype(np.float64) * np.repeat(np.exp2(scales.astype(np.float64) - 127.0), 8, axis=1)[..., None]
    return vals.transpose(0, 1, 3, 2).reshape(g * 512, n)


E2M1 = np.array([0.0, 0.5, 1.0, 1.5, 2.0, 3.0, 4.0, 6.0, -0.0, -0.5, -1.0, -1.5, -2.0, -3.0, -4.0, -6.0])


def pack_fp4(w):
    k, n = w.shape
    w = f64(np.asarray(w, np.float32).astype(ml_dtypes.bfloat16)).reshape(k // 32, 32, n)
    amax = np.abs(w).max(1)
    mant, ex = np.frexp(amax / 6.0)
    byte = np.clip(np.where(amax > 0, np.where(mant > 0.5, ex, ex - 1) + 127, 1), 1, 254)
    scaled = (w * np.exp2(127.0 - byte)[:, None, :]).reshape(k, n).astype(np.float32)
    c = np.ascontiguousarray(scaled.reshape(k // 512, 128, 4, n).transpose(0, 1, 3, 2)).astype(ml_dtypes.float4_e2m1fn).view(np.uint8) & 0xF
    words = (c[..., 0::2] | (c[..., 1::2] << 4)).reshape(k // 512, 128, 2 * n)
    return np.ascontiguousarray(words), np.ascontiguousarray(byte.astype(np.uint8).reshape(k // 512, 16, n))


def unpack_fp4(words, scales):
    g, _, n = scales.shape
    words = np.ascontiguousarray(words).reshape(g, 128, n, 2)
    nib = np.empty((g, 128, n, 4), np.uint8)
    nib[..., 0::2] = words & 0xF
    nib[..., 1::2] = words >> 4
    vals = E2M1[nib] * np.repeat(np.exp2(scales.astype(np.float64) - 127.0), 8, axis=1)[..., None]
    return vals.transpose(0, 1, 3, 2).reshape(g * 512, n)


K, T, S, N, H, U = 512, 2048, 512, 256, 512, 1024


def setup_inputs():
    n = np.random.standard_normal
    s = mx_kscale(K)[:, None]
    u = mx_kscale(H)
    packed_xT = pack_weight(n((K, T)) * s)
    packed_w1 = pack_fp4(n((K, H)) / np.sqrt(K) / s)
    packed_w2 = pack_fp4(n((K, H)) / np.sqrt(K) / s)
    packed_w3 = pack_fp4(n((H, N)) / np.sqrt(H) / u[:, None])
    return {
        "x_words": packed_xT[0],
        "x_scales": packed_xT[1],
        "w1_words": packed_w1[0],
        "w1_scales": packed_w1[1],
        "w2_words": packed_w2[0],
        "w2_scales": packed_w2[1],
        "sca": (np.random.uniform(0.6, 1.4, (H, U))).astype(np.float32),
        "unit": (np.random.uniform(0.6, 1.4, (H, 1)) * u[:, None]).astype(np.float32),
        "w3_words": packed_w3[0],
        "w3_scales": packed_w3[1],
        "offs": striped(np.random.permutation(T)[:S]),
        "va": striped(np.random.permutation(np.concatenate([np.arange(S), np.random.randint(0, S, U - S)]))),
        "vb": striped(np.random.permutation(np.concatenate([np.arange(S), np.random.randint(0, S, U - S)]))),
    }


def reference(x_words, x_scales, w1_words, w1_scales, w2_words, w2_scales, sca, unit, w3_words, w3_scales, offs, va, vb):
    xq = unpack_weight(x_words, x_scales)[:, unstriped(offs)]
    cf = unpack_fp4(w2_words, w2_scales).T @ xq
    conf = np.exp(1.2 * np.tanh(cf)) + 0.5
    ca = conf[:, unstriped(va)]
    cb = conf[:, unstriped(vb)]
    wp = ca * cb
    px = unpack_fp4(w1_words, w1_scales).T @ xq
    xa = px[:, unstriped(va)]
    xb = px[:, unstriped(vb)]
    res = f64(sca) * xa - xb
    hid = f64(unit) * (wp * np.abs(res) - (0.9 * np.log(wp)))
    return unpack_fp4(w3_words, w3_scales).T @ mxq(hid, 0, "e4m3")

@@ -1,0 +1,246 @@
+from contextlib import ExitStack
+
+import concourse.mybir as mybir
+
+K, T, S, N, H, U = 512, 2048, 512, 256, 512, 1024
+FLOPS = 2 * K * H * S * 2 + 2 * H * N * U
+
+F32 = mybir.dt.float32
+BF16 = mybir.dt.bfloat16
+I32 = mybir.dt.int32
+U32 = mybir.dt.uint32
+U16 = mybir.dt.uint16
+U8 = mybir.dt.uint8
+FP8X4 = mybir.dt.float8_e4m3fn_x4
+FP4X4 = mybir.dt.float4_e2m1fn_x4
+ACT = mybir.ActivationFunctionType
+ALU = mybir.AluOpType
+
+P = 128
+PACK = 4
+HALF = 512
+CHUNKS = ((0, 512), (512, 384), (896, 128))
+TINY = 2.0 ** -126
+
+
+def load_scale_rows(nc, plane, rows):
+    for q in range(4):
+        nc.sync.dma_start(out=plane[32 * q : 32 * q + 4, :].bitcast(I32), in_=rows[4 * q : 4 * q + 4, :].bitcast(I32))
+
+
+def deal(nc, out, in_):
+    nc.vector.tensor_copy(out=out.rearrange("p (t m) -> p t m", t=PACK), in_=in_.rearrange("p (m t) -> p t m", t=PACK))
+
+
+def tile_picked_ydustr_loss_p_kernel(
+    tc, x_words, x_scales, w1_words, w1_scales, w2_words, w2_scales, sca, unit, w3_words, w3_scales, offs, va, vb, out
+):
+    nc = tc.nc
+    with ExitStack() as ctx:
+        lists = ctx.enter_context(tc.tile_pool(name="lists", bufs=1))
+        keep = ctx.enter_context(tc.tile_pool(name="keep", bufs=1))
+        psum = ctx.enter_context(tc.psum_pool(name="psum", bufs=1))
+
+        def sb(name, shape, dtype, tag=""):
+            return keep.tile(shape, dtype, name=name, tag=tag or name, align_bytes=64)
+
+        offs_t = lists.tile([P, S // 16], U16, name="offs_t")
+        va_t = lists.tile([P, U // 16], U16, name="va_t")
+        vb_t = lists.tile([P, U // 16], U16, name="vb_t")
+
+        xw = sb("xw", [P, T], U32, "slot_a")
+        xs = sb("xs", [P, T], U8, "slot_b")
+        w1w = sb("w1w", [P, 2 * H], U8, "slot_c")
+        w2w = sb("w2w", [P, 2 * H], U8, "slot_d")
+        w1s = sb("w1s", [P, H], U8)
+        w2s = sb("w2s", [P, H], U8)
+        unit_t = sb("unit_t", [P, PACK], F32)
+
+        nc.gpsimd.memset(xs[:].bitcast(I32), 0)
+        nc.gpsimd.memset(w1s[:].bitcast(I32), 0)
+        nc.gpsimd.memset(w2s[:].bitcast(I32), 0)
+
+        sca_v = sca.rearrange("(p t) r -> p t r", t=PACK)
+        nc.sync.dma_start(offs_t[:], offs)
+        nc.sync.dma_start(out=w1w[:].bitcast(I32), in_=w1_words[0].bitcast(I32))
+        nc.sync.dma_start(out=w2w[:].bitcast(I32), in_=w2_words[0].bitcast(I32))
+        load_scale_rows(nc, xs, x_scales[0])
+        nc.sync.dma_start(out=xw[:].bitcast(I32), in_=x_words[0].rearrange("p n t -> p (n t)").bitcast(I32))
+        load_scale_rows(nc, w1s, w1_scales[0])
+        nc.sync.dma_start(va_t[:], va)
+        nc.sync.dma_start(vb_t[:], vb)
+        nc.sync.dma_start(out=unit_t[:], in_=unit.rearrange("(p t) o -> p (t o)", t=PACK))
+        load_scale_rows(nc, w2s, w2_scales[0])
+
+        w1wd = sb("w1wd", [P, 2 * H], U8)
+        w2wd = sb("w2wd", [P, 2 * H], U8)
+        w1sd = sb("w1sd", [P, H], U8)
+        w2sd = sb("w2sd", [P, H], U8)
+        xqw = sb("xqw", [P, S], U32)
+        xqs = sb("xqs", [P, S], U8)
+        deal(nc, w1wd[:].bitcast(U16), w1w[:].bitcast(U16))
+        deal(nc, w2wd[:].bitcast(U16), w2w[:].bitcast(U16))
+        nc.vector.tensor_copy(out=xqs[:], in_=xs[:].indirect(offs_t[:]))
+        deal(nc, w1sd[:], w1s[:])
+        nc.vector.tensor_copy(out=xqw[:], in_=xw[:].indirect(offs_t[:]))
+        deal(nc, w2sd[:], w2s[:])
+
+        sca_0 = sb("sca_0", [P, U], F32, "slot_d")
+        nc.sync.dma_start(out=sca_0[:], in_=sca_v[:, 0, :])
+        sca_1 = sb("sca_1", [P, U], F32, "slot_b")
+        nc.sync.dma_start(out=sca_1[:], in_=sca_v[:, 1, :])
+        sca_23 = sb("sca_23", [P, 2, U], F32, "slot_a")
+        nc.sync.dma_start(out=sca_23[:], in_=sca_v[:, 2:4, :])
+        sca_t = [sca_0[:], sca_1[:], sca_23[:, 0, :], sca_23[:, 1, :]]
+        w3w = sb("w3w", [P, 2 * N], U8, "slot_c")
+        nc.sync.dma_start(out=w3w[:].bitcast(I32), in_=w3_words[0].bitcast(I32))
+        w3s = w2s[:, :N]
+        load_scale_rows(nc, w3s, w3_scales[0])
+
+        coef = sb("coef", [P, PACK], F32)
+        mag = sb("mag", [P, PACK], F32)
+        den = sb("den", [P, PACK], F32)
+        inv = sb("inv", [P, PACK], F32)
+        nc.scalar.activation(out=coef[:], in_=unit_t[:], func=ACT.Copy, scale=-0.9)
+        nc.scalar.activation(out=mag[:], in_=coef[:], func=ACT.Abs)
+        nc.vector.scalar_tensor_tensor(out=den[:], in0=mag[:], scalar=TINY, in1=coef[:], op0=ALU.is_lt, op1=ALU.add)
+        nc.vector.reciprocal(out=inv[:], in_=den[:])
+
+        def first_product(bank, words, scales, t):
+            acc = psum.tile([P, S], F32, name="acc%d" % bank, tag="bank%d" % bank)
+            nc.tensor.matmul_mx(
+                out=acc[:],
+                lhsT=words[:, 2 * P * t : 2 * P * (t + 1)].bitcast(FP4X4),
+                lhsT_scale=scales[:, P * t : P * (t + 1)],
+                rhs=xqw[:].bitcast(FP8X4),
+                rhs_scale=xqs[:],
+                start=True,
+                stop=True,
+            )
+            return acc
+
+        px_tab = [sb("px_tab%d" % t, [P, 2 * S], F32) for t in range(PACK)]
+        lg_tab = [sb("lg_tab%d" % t, [P, 2 * S], F32) for t in range(PACK)]
+        th = [sb("th%d" % t, [P, S], F32) for t in range(PACK)]
+        ln = [sb("ln%d" % t, [P, S], F32) for t in range(PACK)]
+        px_acc = []
+        cf_acc = []
+        for t in range(PACK):
+            px_acc.append(first_product(2 * t, w1wd, w1sd, t))
+            cf_acc.append(first_product(2 * t + 1, w2wd, w2sd, t))
+        nc.vector.tensor_copy(out=px_tab[0][:, :S], in_=px_acc[0][:])
+        for t in range(PACK):
+            nc.scalar.activation(out=th[t][:], in_=cf_acc[t][:], func=ACT.Tanh)
+            if t + 1 < PACK:
+                nc.scalar.copy(out=px_tab[t + 1][:, :S], in_=px_acc[t + 1][:])
+        for t in range(PACK):
+            nc.scalar.activation(out=lg_tab[t][:, S:], in_=th[t][:], func=ACT.Exp, scale=1.2)
+        for t in range(PACK):
+            nc.scalar.activation(out=ln[t][:], in_=lg_tab[t][:, S:], func=ACT.Ln, bias=0.5)
+        for t in range(PACK):
+            nc.scalar.activation(out=lg_tab[t][:, :S], in_=ln[t][:], func=ACT.Copy, scale=coef[:, t : t + 1])
+
+        def entries(list_tile, r0, n):
+            return list_tile[:, r0 // 16 : (r0 + n) // 16]
+
+        res = {}
+        for t in range(PACK):
+            scaled = [sb("scaled%d_%d" % (t, h), [P, HALF], F32) for h in range(2)]
+            for h in range(2):
+                nc.vector.tensor_tensor(
+                    out=scaled[h][:],
+                    in0=px_tab[t][:].indirect(entries(va_t, h * HALF, HALF)),
+                    in1=sca_t[t][:, h * HALF : (h + 1) * HALF],
+                    op=ALU.mult,
+                )
+            for h in range(2):
+                res[t, h] = sb("res%d_%d" % (t, h), [P, HALF], F32)
+                nc.vector.tensor_tensor(
+                    out=res[t, h][:],
+                    in0=px_tab[t][:].indirect(entries(vb_t, h * HALF, HALF)),
+                    in1=scaled[h][:],
+                    op=ALU.subtract,
+                )
+
+        out_v = out.rearrange("(b p) r -> p b r", p=P)
+        la = {}
+        lw = {}
+        wp = {}
+
+        def gather_a(c):
+            r0, n = CHUNKS[c]
+            for t in range(PACK):
+                la[c, t] = sb("la%d_%d" % (c, t), [P, n], F32)
+                nc.scalar.activation(out=la[c, t][:], in_=lg_tab[t][:].indirect(entries(va_t, r0, n)), func=ACT.Copy)
+
+        def absolute(h):
+            for t in range(PACK):
+                nc.scalar.activation(out=res[t, h][:], in_=res[t, h][:], func=ACT.Abs)
+
+        def gather_b(c):
+            r0, n = CHUNKS[c]
+            lw[c] = sb("lw%d" % c, [P, PACK, n], F32)
+            for t in range(PACK):
+                nc.vector.tensor_tensor(
+                    out=lw[c][:, t, :], in0=lg_tab[t][:].indirect(entries(vb_t, r0, n)), in1=la[c, t][:], op=ALU.add
+                )
+
+        def weights(c):
+            r0, n = CHUNKS[c]
+            for t in range(PACK):
+                wp[c, t] = sb("wp%d_%d" % (c, t), [P, n], F32)
+                nc.scalar.activation(out=wp[c, t][:], in_=lw[c][:, t, :], func=ACT.Exp, scale=inv[:, t : t + 1])
+
+        def finish(c):
+            r0, n = CHUNKS[c]
+            h, c0 = divmod(r0, HALF)
+            term = sb("term%d" % c, [P, PACK, n], F32)
+            for t in range(PACK):
+                nc.vector.scalar_tensor_tensor(
+                    out=term[:, t, :],
+                    in0=res[t, h][:, c0 : c0 + n],
+                    scalar=unit_t[:, t : t + 1],
+                    in1=wp[c, t][:],
+                    op0=ALU.mult,
+                    op1=ALU.mult,
+                )
+            hid = sb("hid%d" % c, [P, n, PACK], BF16)
+            nc.vector.tensor_tensor(
+                out=hid[:].rearrange("p (c i) t -> p c t i", i=4),
+                in0=term[:].rearrange("p t (c i) -> p c t i", i=4),
+                in1=lw[c][:].rearrange("p t (c i) -> p c t i", i=4),
+                op=ALU.add,
+            )
+            codes = sb("codes%d" % c, [P, n], U32)
+            plane = sb("plane%d" % c, [P, n], U8)
+            nc.vector.quantize_mx(out=codes[:].bitcast(FP8X4), scales=plane[:], in_=hid[:].rearrange("p r t -> p (r t)"))
+            result = sb("result%d" % c, [P, 2, n], F32)
+            for b in range(2):
+                acc = psum.tile([P, n], F32, name="out%d_%d" % (c, b), tag="bank%d" % (2 * c + b))
+                for n0, nn in ((0, 256), (256, 128)) if n == 384 else ((0, n),):
+                    nc.tensor.matmul_mx(
+                        out=acc[:, n0 : n0 + nn],
+                        lhsT=w3w[:, 2 * P * b : 2 * P * (b + 1)].bitcast(FP4X4),
+                        lhsT_scale=w3s[:, P * b : P * (b + 1)],
+                        rhs=codes[:, n0 : n0 + nn].bitcast(FP8X4),
+                        rhs_scale=plane[:, n0 : n0 + nn],
+                        start=True,
+                        stop=True,
+                    )
+                nc.scalar.copy(out=result[:, b, :], in_=acc[:])
+            nc.sync.dma_start(out=out_v[:, :, r0 : r0 + n], in_=result[:])
+
+        gather_a(0)
+        absolute(0)
+        gather_b(0)
+        gather_a(1)
+        weights(0)
+        gather_a(2)
+        absolute(1)
+        gather_b(1)
+        finish(0)
+        weights(1)
+        gather_b(2)
+        weights(2)
+        finish(1)
+        finish(2)

@@ -23,9 +23,9 @@ CHUNKS = ((0, 512), (512, 384), (896, 128))
 TINY = 2.0 ** -126
 
 
-def load_scale_rows(nc, plane, rows):
-    for q in range(4):
-        nc.sync.dma_start(out=plane[32 * q : 32 * q + 4, :].bitcast(I32), in_=rows[4 * q : 4 * q + 4, :].bitcast(I32))
+def load_scale_rows(queue, plane, rows, quadrants):
+    for q in quadrants:
+        queue.dma_start(out=plane[32 * q : 32 * q + 4, :].bitcast(I32), in_=rows[4 * q : 4 * q + 4, :].bitcast(I32))
 
 
 def deal(nc, out, in_):
@@ -39,6 +39,7 @@ def tile_picked_ydustr_loss_p_kernel(
     with ExitStack() as ctx:
         lists = ctx.enter_context(tc.tile_pool(name="lists", bufs=1))
         keep = ctx.enter_context(tc.tile_pool(name="keep", bufs=1))
+        head = ctx.enter_context(tc.tile_pool(name="head", bufs=1))
         psum = ctx.enter_context(tc.psum_pool(name="psum", bufs=1))
 
         def sb(name, shape, dtype, tag=""):
@@ -49,71 +50,74 @@ def tile_picked_ydustr_loss_p_kernel(
         vb_t = lists.tile([P, U // 16], U16, name="vb_t")
 
         xw = sb("xw", [P, T], U32, "slot_a")
-        xs = sb("xs", [P, T], U8, "slot_b")
+        xs = head.tile([P, T], U8, name="xs", align_bytes=64, offset=3136)
         w1w = sb("w1w", [P, 2 * H], U8, "slot_c")
-        w2w = sb("w2w", [P, 2 * H], U8, "slot_d")
-        w1s = sb("w1s", [P, H], U8)
-        w2s = sb("w2s", [P, H], U8)
-        unit_t = sb("unit_t", [P, PACK], F32)
+        ws = sb("ws", [P, H], U8)
 
-        nc.gpsimd.memset(xs[:].bitcast(I32), 0)
-        nc.gpsimd.memset(w1s[:].bitcast(I32), 0)
-        nc.gpsimd.memset(w2s[:].bitcast(I32), 0)
+        nc.gpsimd.memset(ws[:].bitcast(I32), 0)
+        nc.vector.memset(xs[:].bitcast(I32), 0)
 
-        sca_v = sca.rearrange("(p t) r -> p t r", t=PACK)
+        sca_v = sca.rearrange("(p t) r -> p (t r)", t=PACK)
         nc.sync.dma_start(offs_t[:], offs)
         nc.sync.dma_start(out=w1w[:].bitcast(I32), in_=w1_words[0].bitcast(I32))
-        nc.sync.dma_start(out=w2w[:].bitcast(I32), in_=w2_words[0].bitcast(I32))
-        load_scale_rows(nc, xs, x_scales[0])
-        nc.sync.dma_start(out=xw[:].bitcast(I32), in_=x_words[0].rearrange("p n t -> p (n t)").bitcast(I32))
-        load_scale_rows(nc, w1s, w1_scales[0])
         nc.sync.dma_start(va_t[:], va)
+        nc.sync.dma_start(out=xw[:].bitcast(I32), in_=x_words[0].rearrange("p n t -> p (n t)").bitcast(I32))
         nc.sync.dma_start(vb_t[:], vb)
-        nc.sync.dma_start(out=unit_t[:], in_=unit.rearrange("(p t) o -> p (t o)", t=PACK))
-        load_scale_rows(nc, w2s, w2_scales[0])
+        load_scale_rows(nc.scalar, xs, x_scales[0], range(4))
+        load_scale_rows(nc.scalar, ws, w1_scales[0], range(2))
+        load_scale_rows(nc.gpsimd, ws, w1_scales[0], range(2, 4))
 
         w1wd = sb("w1wd", [P, 2 * H], U8)
         w2wd = sb("w2wd", [P, 2 * H], U8)
         w1sd = sb("w1sd", [P, H], U8)
         w2sd = sb("w2sd", [P, H], U8)
-        xqw = sb("xqw", [P, S], U32)
+        xqw = head.tile([P, S], U32, name="xqw", align_bytes=64, offset=4160)
         xqs = sb("xqs", [P, S], U8)
         deal(nc, w1wd[:].bitcast(U16), w1w[:].bitcast(U16))
-        deal(nc, w2wd[:].bitcast(U16), w2w[:].bitcast(U16))
         nc.vector.tensor_copy(out=xqs[:], in_=xs[:].indirect(offs_t[:]))
-        deal(nc, w1sd[:], w1s[:])
-        nc.vector.tensor_copy(out=xqw[:], in_=xw[:].indirect(offs_t[:]))
-        deal(nc, w2sd[:], w2s[:])
+        deal(nc, w1sd[:], ws[:])
+        nc.vector.tensor_copy(out=xqw[:, :256], in_=xw[:].indirect(offs_t[:, :16]))
+        nc.vector.tensor_copy(out=xqw[:, 256:], in_=xw[:].indirect(offs_t[:, 16:]))
 
-        sca_0 = sb("sca_0", [P, U], F32, "slot_d")
-        nc.sync.dma_start(out=sca_0[:], in_=sca_v[:, 0, :])
-        sca_1 = sb("sca_1", [P, U], F32, "slot_b")
-        nc.sync.dma_start(out=sca_1[:], in_=sca_v[:, 1, :])
-        sca_23 = sb("sca_23", [P, 2, U], F32, "slot_a")
-        nc.sync.dma_start(out=sca_23[:], in_=sca_v[:, 2:4, :])
-        sca_t = [sca_0[:], sca_1[:], sca_23[:, 0, :], sca_23[:, 1, :]]
+        early = head.tile([P, U + PACK], F32, name="early", align_bytes=64, offset=0)
+        for h in range(2):
+            nc.sync.dma_start(out=early[:, h * HALF : (h + 1) * HALF], in_=sca_v[:, h * HALF : (h + 1) * HALF])
+        w2w = sb("w2w", [P, 2 * H], U8, "slot_c")
+        nc.sync.dma_start(out=w2w[:].bitcast(I32), in_=w2_words[0].bitcast(I32))
+        load_scale_rows(nc.sync, ws, w2_scales[0], range(4))
+        deal(nc, w2wd[:].bitcast(U16), w2w[:].bitcast(U16))
+        deal(nc, w2sd[:], ws[:])
+        late = sb("late", [P, (PACK - 1) * U], F32, "slot_a")
+        for c0, c1 in ((U, 2 * U), (2 * U, 4 * U)):
+            nc.sync.dma_start(out=late[:, c0 - U : c1 - U], in_=sca_v[:, c0:c1])
+        unit_t = early[:, U:]
+        nc.sync.dma_start(out=unit_t, in_=unit.rearrange("(p t) o -> p (t o)", t=PACK))
         w3w = sb("w3w", [P, 2 * N], U8, "slot_c")
         nc.sync.dma_start(out=w3w[:].bitcast(I32), in_=w3_words[0].bitcast(I32))
-        w3s = w2s[:, :N]
-        load_scale_rows(nc, w3s, w3_scales[0])
+        w3s = ws[:, :N]
+        load_scale_rows(nc.sync, w3s, w3_scales[0], range(4))
+
+        def sca_half(t, h):
+            c0 = (t - 1) * U + h * HALF
+            return late[:, c0 : c0 + HALF] if t else early[:, h * HALF : (h + 1) * HALF]
 
         coef = sb("coef", [P, PACK], F32)
         mag = sb("mag", [P, PACK], F32)
         den = sb("den", [P, PACK], F32)
         inv = sb("inv", [P, PACK], F32)
-        nc.scalar.activation(out=coef[:], in_=unit_t[:], func=ACT.Copy, scale=-0.9)
+        nc.scalar.activation(out=coef[:], in_=unit_t, func=ACT.Copy, scale=-0.9)
         nc.scalar.activation(out=mag[:], in_=coef[:], func=ACT.Abs)
         nc.vector.scalar_tensor_tensor(out=den[:], in0=mag[:], scalar=TINY, in1=coef[:], op0=ALU.is_lt, op1=ALU.add)
         nc.vector.reciprocal(out=inv[:], in_=den[:])
 
-        def first_product(bank, words, scales, t):
-            acc = psum.tile([P, S], F32, name="acc%d" % bank, tag="bank%d" % bank)
+        def first_product(bank, words, scales, t, c0, n):
+            acc = psum.tile([P, n], F32, name="acc%d_%d" % (bank, c0), tag="bank%d" % bank)
             nc.tensor.matmul_mx(
                 out=acc[:],
                 lhsT=words[:, 2 * P * t : 2 * P * (t + 1)].bitcast(FP4X4),
                 lhsT_scale=scales[:, P * t : P * (t + 1)],
-                rhs=xqw[:].bitcast(FP8X4),
-                rhs_scale=xqs[:],
+                rhs=xqw[:, c0 : c0 + n].bitcast(FP8X4),
+                rhs_scale=xqs[:, c0 : c0 + n],
                 start=True,
                 stop=True,
             )
@@ -123,16 +127,15 @@ def tile_picked_ydustr_loss_p_kernel(
         lg_tab = [sb("lg_tab%d" % t, [P, 2 * S], F32) for t in range(PACK)]
         th = [sb("th%d" % t, [P, S], F32) for t in range(PACK)]
         ln = [sb("ln%d" % t, [P, S], F32) for t in range(PACK)]
-        px_acc = []
-        cf_acc = []
+        for h in range(2):
+            acc = first_product(7 * h, w1wd, w1sd, 0, 256 * h, 256)
+            nc.vector.tensor_copy(out=px_tab[0][:, 256 * h : 256 * (h + 1)], in_=acc[:])
         for t in range(PACK):
-            px_acc.append(first_product(2 * t, w1wd, w1sd, t))
-            cf_acc.append(first_product(2 * t + 1, w2wd, w2sd, t))
-        nc.vector.tensor_copy(out=px_tab[0][:, :S], in_=px_acc[0][:])
-        for t in range(PACK):
-            nc.scalar.activation(out=th[t][:], in_=cf_acc[t][:], func=ACT.Tanh)
             if t + 1 < PACK:
-                nc.scalar.copy(out=px_tab[t + 1][:, :S], in_=px_acc[t + 1][:])
+                acc = first_product(2 * t + 2, w1wd, w1sd, t + 1, 0, S)
+                nc.scalar.copy(out=px_tab[t + 1][:, :S], in_=acc[:])
+            acc = first_product(2 * t + 1, w2wd, w2sd, t, 0, S)
+            nc.scalar.activation(out=th[t][:], in_=acc[:], func=ACT.Tanh)
         for t in range(PACK):
             nc.scalar.activation(out=lg_tab[t][:, S:], in_=th[t][:], func=ACT.Exp, scale=1.2)
         for t in range(PACK):
@@ -150,7 +153,7 @@ def tile_picked_ydustr_loss_p_kernel(
                 nc.vector.tensor_tensor(
                     out=scaled[h][:],
                     in0=px_tab[t][:].indirect(entries(va_t, h * HALF, HALF)),
-                    in1=sca_t[t][:, h * HALF : (h + 1) * HALF],
+                    in1=sca_half(t, h),
                     op=ALU.mult,
                 )
             for h in range(2):
@@ -169,9 +172,9 @@ def tile_picked_ydustr_loss_p_kernel(
 
         def gather_a(c):
             r0, n = CHUNKS[c]
+            la[c] = sb("la%d" % c, [P, PACK, n], F32)
             for t in range(PACK):
-                la[c, t] = sb("la%d_%d" % (c, t), [P, n], F32)
-                nc.scalar.activation(out=la[c, t][:], in_=lg_tab[t][:].indirect(entries(va_t, r0, n)), func=ACT.Copy)
+                nc.scalar.activation(out=la[c][:, t, :], in_=lg_tab[t][:].indirect(entries(va_t, r0, n)), func=ACT.Copy)
 
         def absolute(h):
             for t in range(PACK):
@@ -182,8 +185,16 @@ def tile_picked_ydustr_loss_p_kernel(
             lw[c] = sb("lw%d" % c, [P, PACK, n], F32)
             for t in range(PACK):
                 nc.vector.tensor_tensor(
-                    out=lw[c][:, t, :], in0=lg_tab[t][:].indirect(entries(vb_t, r0, n)), in1=la[c, t][:], op=ALU.add
+                    out=lw[c][:, t, :], in0=lg_tab[t][:].indirect(entries(vb_t, r0, n)), in1=la[c][:, t, :], op=ALU.add
                 )
+
+        def gather_b_apart(c):
+            r0, n = CHUNKS[c]
+            lb = sb("lb%d" % c, [P, PACK, n], F32)
+            lw[c] = sb("lw%d" % c, [P, PACK, n], F32)
+            for t in range(PACK):
+                nc.scalar.activation(out=lb[:, t, :], in_=lg_tab[t][:].indirect(entries(vb_t, r0, n)), func=ACT.Copy)
+            nc.vector.tensor_tensor(out=lw[c][:], in0=lb[:], in1=la[c][:], op=ALU.add)
 
         def weights(c):
             r0, n = CHUNKS[c]
@@ -227,7 +238,10 @@ def tile_picked_ydustr_loss_p_kernel(
                         start=True,
                         stop=True,
                     )
-                nc.scalar.copy(out=result[:, b, :], in_=acc[:])
+                if c == 2 and b == 1:
+                    nc.vector.tensor_copy(out=result[:, b, :], in_=acc[:])
+                else:
+                    nc.scalar.copy(out=result[:, b, :], in_=acc[:])
             nc.sync.dma_start(out=out_v[:, :, r0 : r0 + n], in_=result[:])
 
         gather_a(0)
@@ -240,7 +254,7 @@ def tile_picked_ydustr_loss_p_kernel(
         gather_b(1)
         finish(0)
         weights(1)
-        gather_b(2)
+        gather_b_apart(2)
         weights(2)
         finish(1)
         finish(2)

@@ -39,7 +39,6 @@ def tile_picked_ydustr_loss_p_kernel(
     with ExitStack() as ctx:
         lists = ctx.enter_context(tc.tile_pool(name="lists", bufs=1))
         keep = ctx.enter_context(tc.tile_pool(name="keep", bufs=1))
-        head = ctx.enter_context(tc.tile_pool(name="head", bufs=1))
         psum = ctx.enter_context(tc.psum_pool(name="psum", bufs=1))
 
         def sb(name, shape, dtype, tag=""):
@@ -49,57 +48,60 @@ def tile_picked_ydustr_loss_p_kernel(
         va_t = lists.tile([P, U // 16], U16, name="va_t")
         vb_t = lists.tile([P, U // 16], U16, name="vb_t")
 
-        xw = sb("xw", [P, T], U32, "slot_a")
-        xs = head.tile([P, T], U8, name="xs", align_bytes=64, offset=3136)
-        w1w = sb("w1w", [P, 2 * H], U8, "slot_c")
-        ws = sb("ws", [P, H], U8)
+        xw = sb("xw", [P, T], U32)
+        xs = sb("xs", [P, T], U8)
+        w1w = sb("w1w", [P, 2 * H], U8)
+        w2w = sb("w2w", [P, 2 * H], U8)
+        w3w = sb("w3w", [P, 2 * N], U8)
+        w1s = sb("w1s", [P, H], U8)
+        w2s = sb("w2s", [P, H], U8)
+        unit_t = sb("unit_t", [P, PACK], F32)[:]
+        sca_t = sb("sca_t", [P, PACK * U], F32)
 
-        nc.gpsimd.memset(ws[:].bitcast(I32), 0)
-        nc.vector.memset(xs[:].bitcast(I32), 0)
+        nc.gpsimd.memset(xs[:].bitcast(I32), 0)
+        nc.gpsimd.memset(w1s[:].bitcast(I32), 0)
+        nc.gpsimd.memset(w2s[:].bitcast(I32), 0)
 
         sca_v = sca.rearrange("(p t) r -> p (t r)", t=PACK)
+
+        def load_sca(c0, c1):
+            nc.sync.dma_start(out=sca_t[:, c0:c1], in_=sca_v[:, c0:c1])
+
         nc.sync.dma_start(offs_t[:], offs)
         nc.sync.dma_start(out=w1w[:].bitcast(I32), in_=w1_words[0].bitcast(I32))
-        nc.sync.dma_start(va_t[:], va)
+        nc.sync.dma_start(out=w2w[:].bitcast(I32), in_=w2_words[0].bitcast(I32))
+        load_scale_rows(nc.sync, xs, x_scales[0], range(4))
         nc.sync.dma_start(out=xw[:].bitcast(I32), in_=x_words[0].rearrange("p n t -> p (n t)").bitcast(I32))
+        load_scale_rows(nc.sync, w1s, w1_scales[0], range(4))
+        load_scale_rows(nc.sync, w2s, w2_scales[0], range(3))
+        load_sca(0, HALF)
+        load_scale_rows(nc.sync, w2s, w2_scales[0], range(3, 4))
+        nc.sync.dma_start(va_t[:], va)
         nc.sync.dma_start(vb_t[:], vb)
-        load_scale_rows(nc.scalar, xs, x_scales[0], range(4))
-        load_scale_rows(nc.scalar, ws, w1_scales[0], range(2))
-        load_scale_rows(nc.gpsimd, ws, w1_scales[0], range(2, 4))
+        load_sca(HALF, U)
+        nc.sync.dma_start(out=unit_t, in_=unit.rearrange("(p t) o -> p (t o)", t=PACK))
+        load_sca(U, 2 * U)
+        load_sca(2 * U, 4 * U)
+        nc.sync.dma_start(out=w3w[:].bitcast(I32), in_=w3_words[0].bitcast(I32))
 
         w1wd = sb("w1wd", [P, 2 * H], U8)
         w2wd = sb("w2wd", [P, 2 * H], U8)
         w1sd = sb("w1sd", [P, H], U8)
         w2sd = sb("w2sd", [P, H], U8)
-        xqw = head.tile([P, S], U32, name="xqw", align_bytes=64, offset=4160)
+        xqw = sb("xqw", [P, S], U32)
         xqs = sb("xqs", [P, S], U8)
         deal(nc, w1wd[:].bitcast(U16), w1w[:].bitcast(U16))
+        deal(nc, w2wd[:].bitcast(U16), w2w[:].bitcast(U16))
         nc.vector.tensor_copy(out=xqs[:], in_=xs[:].indirect(offs_t[:]))
-        deal(nc, w1sd[:], ws[:])
+        deal(nc, w1sd[:], w1s[:])
         nc.vector.tensor_copy(out=xqw[:, :256], in_=xw[:].indirect(offs_t[:, :16]))
         nc.vector.tensor_copy(out=xqw[:, 256:], in_=xw[:].indirect(offs_t[:, 16:]))
-
-        early = head.tile([P, U + PACK], F32, name="early", align_bytes=64, offset=0)
-        for h in range(2):
-            nc.sync.dma_start(out=early[:, h * HALF : (h + 1) * HALF], in_=sca_v[:, h * HALF : (h + 1) * HALF])
-        w2w = sb("w2w", [P, 2 * H], U8, "slot_c")
-        nc.sync.dma_start(out=w2w[:].bitcast(I32), in_=w2_words[0].bitcast(I32))
-        load_scale_rows(nc.sync, ws, w2_scales[0], range(4))
-        deal(nc, w2wd[:].bitcast(U16), w2w[:].bitcast(U16))
-        deal(nc, w2sd[:], ws[:])
-        late = sb("late", [P, (PACK - 1) * U], F32, "slot_a")
-        for c0, c1 in ((U, 2 * U), (2 * U, 4 * U)):
-            nc.sync.dma_start(out=late[:, c0 - U : c1 - U], in_=sca_v[:, c0:c1])
-        unit_t = early[:, U:]
-        nc.sync.dma_start(out=unit_t, in_=unit.rearrange("(p t) o -> p (t o)", t=PACK))
-        w3w = sb("w3w", [P, 2 * N], U8, "slot_c")
-        nc.sync.dma_start(out=w3w[:].bitcast(I32), in_=w3_words[0].bitcast(I32))
-        w3s = ws[:, :N]
+        deal(nc, w2sd[:], w2s[:])
+        w3s = w1s[:, :N]
         load_scale_rows(nc.sync, w3s, w3_scales[0], range(4))
 
         def sca_half(t, h):
-            c0 = (t - 1) * U + h * HALF
-            return late[:, c0 : c0 + HALF] if t else early[:, h * HALF : (h + 1) * HALF]
+            return sca_t[:, t * U + h * HALF : t * U + (h + 1) * HALF]
 
         coef = sb("coef", [P, PACK], F32)
         mag = sb("mag", [P, PACK], F32)
@@ -188,13 +190,19 @@ def tile_picked_ydustr_loss_p_kernel(
                     out=lw[c][:, t, :], in0=lg_tab[t][:].indirect(entries(vb_t, r0, n)), in1=la[c][:, t, :], op=ALU.add
                 )
 
-        def gather_b_apart(c):
+        lb = {}
+        terms = {}
+
+        def gather_b_plain(c):
             r0, n = CHUNKS[c]
-            lb = sb("lb%d" % c, [P, PACK, n], F32)
-            lw[c] = sb("lw%d" % c, [P, PACK, n], F32)
+            lb[c] = sb("lb%d" % c, [P, PACK, n], F32)
             for t in range(PACK):
-                nc.scalar.activation(out=lb[:, t, :], in_=lg_tab[t][:].indirect(entries(vb_t, r0, n)), func=ACT.Copy)
-            nc.vector.tensor_tensor(out=lw[c][:], in0=lb[:], in1=la[c][:], op=ALU.add)
+                nc.scalar.activation(out=lb[c][:, t, :], in_=lg_tab[t][:].indirect(entries(vb_t, r0, n)), func=ACT.Copy)
+
+        def add_logs(c):
+            r0, n = CHUNKS[c]
+            lw[c] = sb("lw%d" % c, [P, PACK, n], F32)
+            nc.vector.tensor_tensor(out=lw[c][:], in0=lb[c][:], in1=la[c][:], op=ALU.add)
 
         def weights(c):
             r0, n = CHUNKS[c]
@@ -202,10 +210,11 @@ def tile_picked_ydustr_loss_p_kernel(
                 wp[c, t] = sb("wp%d_%d" % (c, t), [P, n], F32)
                 nc.scalar.activation(out=wp[c, t][:], in_=lw[c][:, t, :], func=ACT.Exp, scale=inv[:, t : t + 1])
 
-        def finish(c):
+        def weigh(c):
             r0, n = CHUNKS[c]
             h, c0 = divmod(r0, HALF)
             term = sb("term%d" % c, [P, PACK, n], F32)
+            terms[c] = term
             for t in range(PACK):
                 nc.vector.scalar_tensor_tensor(
                     out=term[:, t, :],
@@ -215,6 +224,10 @@ def tile_picked_ydustr_loss_p_kernel(
                     op0=ALU.mult,
                     op1=ALU.mult,
                 )
+
+        def finish(c):
+            r0, n = CHUNKS[c]
+            term = terms[c]
             hid = sb("hid%d" % c, [P, n, PACK], BF16)
             nc.vector.tensor_tensor(
                 out=hid[:].rearrange("p (c i) t -> p c t i", i=4),
@@ -249,12 +262,16 @@ def tile_picked_ydustr_loss_p_kernel(
         gather_b(0)
         gather_a(1)
         weights(0)
-        gather_a(2)
-        absolute(1)
         gather_b(1)
-        finish(0)
         weights(1)
-        gather_b_apart(2)
+        absolute(1)
+        weigh(0)
+        gather_a(2)
+        gather_b_plain(2)
+        finish(0)
+        weigh(1)
+        add_logs(2)
         weights(2)
         finish(1)
+        weigh(2)
         finish(2)

from contextlib import ExitStack

import concourse.mybir as mybir

K, T, S, N, H, U = 512, 2048, 512, 256, 512, 1024
FLOPS = 2 * K * H * S * 2 + 2 * H * N * U

F32 = mybir.dt.float32
BF16 = mybir.dt.bfloat16
I32 = mybir.dt.int32
U32 = mybir.dt.uint32
U16 = mybir.dt.uint16
U8 = mybir.dt.uint8
FP8X4 = mybir.dt.float8_e4m3fn_x4
FP4X4 = mybir.dt.float4_e2m1fn_x4
ACT = mybir.ActivationFunctionType
ALU = mybir.AluOpType

P = 128
PACK = 4
HALF = 512
CHUNKS = ((0, 512), (512, 384), (896, 128))
TINY = 2.0 ** -126


def load_scale_rows(queue, plane, rows, quadrants):
    for q in quadrants:
        queue.dma_start(out=plane[32 * q : 32 * q + 4, :].bitcast(I32), in_=rows[4 * q : 4 * q + 4, :].bitcast(I32))


def deal(nc, out, in_):
    nc.vector.tensor_copy(out=out.rearrange("p (t m) -> p t m", t=PACK), in_=in_.rearrange("p (m t) -> p t m", t=PACK))


def tile_picked_ydustr_loss_p_kernel(
    tc, x_words, x_scales, w1_words, w1_scales, w2_words, w2_scales, sca, unit, w3_words, w3_scales, offs, va, vb, out
):
    nc = tc.nc
    with ExitStack() as ctx:
        lists = ctx.enter_context(tc.tile_pool(name="lists", bufs=1))
        keep = ctx.enter_context(tc.tile_pool(name="keep", bufs=1))
        psum = ctx.enter_context(tc.psum_pool(name="psum", bufs=1))

        def sb(name, shape, dtype, tag=""):
            return keep.tile(shape, dtype, name=name, tag=tag or name, align_bytes=64)

        offs_t = lists.tile([P, S // 16], U16, name="offs_t")
        va_t = lists.tile([P, U // 16], U16, name="va_t")
        vb_t = lists.tile([P, U // 16], U16, name="vb_t")

        xw = sb("xw", [P, T], U32)
        xs = sb("xs", [P, T], U8)
        w1w = sb("w1w", [P, 2 * H], U8)
        w2w = sb("w2w", [P, 2 * H], U8)
        w3w = sb("w3w", [P, 2 * N], U8)
        w1s = sb("w1s", [P, H], U8)
        w2s = sb("w2s", [P, H], U8)
        unit_t = sb("unit_t", [P, PACK], F32)[:]
        sca_t = sb("sca_t", [P, PACK * U], F32)

        nc.gpsimd.memset(xs[:].bitcast(I32), 0)
        nc.gpsimd.memset(w1s[:].bitcast(I32), 0)
        nc.gpsimd.memset(w2s[:].bitcast(I32), 0)

        sca_v = sca.rearrange("(p t) r -> p (t r)", t=PACK)

        def load_sca(c0, c1):
            nc.sync.dma_start(out=sca_t[:, c0:c1], in_=sca_v[:, c0:c1])

        nc.sync.dma_start(offs_t[:], offs)
        nc.sync.dma_start(out=w1w[:].bitcast(I32), in_=w1_words[0].bitcast(I32))
        nc.sync.dma_start(out=w2w[:].bitcast(I32), in_=w2_words[0].bitcast(I32))
        load_scale_rows(nc.sync, xs, x_scales[0], range(4))
        nc.sync.dma_start(out=xw[:].bitcast(I32), in_=x_words[0].rearrange("p n t -> p (n t)").bitcast(I32))
        load_scale_rows(nc.sync, w1s, w1_scales[0], range(4))
        load_scale_rows(nc.sync, w2s, w2_scales[0], range(3))
        load_sca(0, HALF)
        load_scale_rows(nc.sync, w2s, w2_scales[0], range(3, 4))
        nc.sync.dma_start(va_t[:], va)
        nc.sync.dma_start(vb_t[:], vb)
        load_sca(HALF, U)
        nc.sync.dma_start(out=unit_t, in_=unit.rearrange("(p t) o -> p (t o)", t=PACK))
        load_sca(U, 2 * U)
        load_sca(2 * U, 4 * U)
        nc.sync.dma_start(out=w3w[:].bitcast(I32), in_=w3_words[0].bitcast(I32))

        w1wd = sb("w1wd", [P, 2 * H], U8)
        w2wd = sb("w2wd", [P, 2 * H], U8)
        w1sd = sb("w1sd", [P, H], U8)
        w2sd = sb("w2sd", [P, H], U8)
        xqw = sb("xqw", [P, S], U32)
        xqs = sb("xqs", [P, S], U8)
        deal(nc, w1wd[:].bitcast(U16), w1w[:].bitcast(U16))
        deal(nc, w2wd[:].bitcast(U16), w2w[:].bitcast(U16))
        nc.vector.tensor_copy(out=xqs[:], in_=xs[:].indirect(offs_t[:]))
        deal(nc, w1sd[:], w1s[:])
        nc.vector.tensor_copy(out=xqw[:, :256], in_=xw[:].indirect(offs_t[:, :16]))
        nc.vector.tensor_copy(out=xqw[:, 256:], in_=xw[:].indirect(offs_t[:, 16:]))
        deal(nc, w2sd[:], w2s[:])
        w3s = w1s[:, :N]
        load_scale_rows(nc.sync, w3s, w3_scales[0], range(4))

        def sca_half(t, h):
            return sca_t[:, t * U + h * HALF : t * U + (h + 1) * HALF]

        coef = sb("coef", [P, PACK], F32)
        mag = sb("mag", [P, PACK], F32)
        den = sb("den", [P, PACK], F32)
        inv = sb("inv", [P, PACK], F32)
        nc.scalar.activation(out=coef[:], in_=unit_t, func=ACT.Copy, scale=-0.9)
        nc.scalar.activation(out=mag[:], in_=coef[:], func=ACT.Abs)
        nc.vector.scalar_tensor_tensor(out=den[:], in0=mag[:], scalar=TINY, in1=coef[:], op0=ALU.is_lt, op1=ALU.add)
        nc.vector.reciprocal(out=inv[:], in_=den[:])

        def first_product(bank, words, scales, t, c0, n):
            acc = psum.tile([P, n], F32, name="acc%d_%d" % (bank, c0), tag="bank%d" % bank)
            nc.tensor.matmul_mx(
                out=acc[:],
                lhsT=words[:, 2 * P * t : 2 * P * (t + 1)].bitcast(FP4X4),
                lhsT_scale=scales[:, P * t : P * (t + 1)],
                rhs=xqw[:, c0 : c0 + n].bitcast(FP8X4),
                rhs_scale=xqs[:, c0 : c0 + n],
                start=True,
                stop=True,
            )
            return acc

        px_tab = [sb("px_tab%d" % t, [P, 2 * S], F32) for t in range(PACK)]
        lg_tab = [sb("lg_tab%d" % t, [P, 2 * S], F32) for t in range(PACK)]
        th = [sb("th%d" % t, [P, S], F32) for t in range(PACK)]
        ln = [sb("ln%d" % t, [P, S], F32) for t in range(PACK)]
        for h in range(2):
            acc = first_product(7 * h, w1wd, w1sd, 0, 256 * h, 256)
            nc.vector.tensor_copy(out=px_tab[0][:, 256 * h : 256 * (h + 1)], in_=acc[:])
        for t in range(PACK):
            if t + 1 < PACK:
                acc = first_product(2 * t + 2, w1wd, w1sd, t + 1, 0, S)
                nc.scalar.copy(out=px_tab[t + 1][:, :S], in_=acc[:])
            acc = first_product(2 * t + 1, w2wd, w2sd, t, 0, S)
            nc.scalar.activation(out=th[t][:], in_=acc[:], func=ACT.Tanh)
        for t in range(PACK):
            nc.scalar.activation(out=lg_tab[t][:, S:], in_=th[t][:], func=ACT.Exp, scale=1.2)
        for t in range(PACK):
            nc.scalar.activation(out=ln[t][:], in_=lg_tab[t][:, S:], func=ACT.Ln, bias=0.5)
        for t in range(PACK):
            nc.scalar.activation(out=lg_tab[t][:, :S], in_=ln[t][:], func=ACT.Copy, scale=coef[:, t : t + 1])

        def entries(list_tile, r0, n):
            return list_tile[:, r0 // 16 : (r0 + n) // 16]

        res = {}
        for t in range(PACK):
            scaled = [sb("scaled%d_%d" % (t, h), [P, HALF], F32) for h in range(2)]
            for h in range(2):
                nc.vector.tensor_tensor(
                    out=scaled[h][:],
                    in0=px_tab[t][:].indirect(entries(va_t, h * HALF, HALF)),
                    in1=sca_half(t, h),
                    op=ALU.mult,
                )
            for h in range(2):
                res[t, h] = sb("res%d_%d" % (t, h), [P, HALF], F32)
                nc.vector.tensor_tensor(
                    out=res[t, h][:],
                    in0=px_tab[t][:].indirect(entries(vb_t, h * HALF, HALF)),
                    in1=scaled[h][:],
                    op=ALU.subtract,
                )

        out_v = out.rearrange("(b p) r -> p b r", p=P)
        la = {}
        lw = {}
        wp = {}

        def gather_a(c):
            r0, n = CHUNKS[c]
            la[c] = sb("la%d" % c, [P, PACK, n], F32)
            for t in range(PACK):
                nc.scalar.activation(out=la[c][:, t, :], in_=lg_tab[t][:].indirect(entries(va_t, r0, n)), func=ACT.Copy)

        def absolute(h):
            for t in range(PACK):
                nc.scalar.activation(out=res[t, h][:], in_=res[t, h][:], func=ACT.Abs)

        def gather_b(c):
            r0, n = CHUNKS[c]
            lw[c] = sb("lw%d" % c, [P, PACK, n], F32)
            for t in range(PACK):
                nc.vector.tensor_tensor(
                    out=lw[c][:, t, :], in0=lg_tab[t][:].indirect(entries(vb_t, r0, n)), in1=la[c][:, t, :], op=ALU.add
                )

        lb = {}
        terms = {}

        def gather_b_plain(c):
            r0, n = CHUNKS[c]
            lb[c] = sb("lb%d" % c, [P, PACK, n], F32)
            for t in range(PACK):
                nc.scalar.activation(out=lb[c][:, t, :], in_=lg_tab[t][:].indirect(entries(vb_t, r0, n)), func=ACT.Copy)

        def add_logs(c):
            r0, n = CHUNKS[c]
            lw[c] = sb("lw%d" % c, [P, PACK, n], F32)
            nc.vector.tensor_tensor(out=lw[c][:], in0=lb[c][:], in1=la[c][:], op=ALU.add)

        def weights(c):
            r0, n = CHUNKS[c]
            for t in range(PACK):
                wp[c, t] = sb("wp%d_%d" % (c, t), [P, n], F32)
                nc.scalar.activation(out=wp[c, t][:], in_=lw[c][:, t, :], func=ACT.Exp, scale=inv[:, t : t + 1])

        def weigh(c):
            r0, n = CHUNKS[c]
            h, c0 = divmod(r0, HALF)
            term = sb("term%d" % c, [P, PACK, n], F32)
            terms[c] = term
            for t in range(PACK):
                nc.vector.scalar_tensor_tensor(
                    out=term[:, t, :],
                    in0=res[t, h][:, c0 : c0 + n],
                    scalar=unit_t[:, t : t + 1],
                    in1=wp[c, t][:],
                    op0=ALU.mult,
                    op1=ALU.mult,
                )

        def finish(c):
            r0, n = CHUNKS[c]
            term = terms[c]
            hid = sb("hid%d" % c, [P, n, PACK], BF16)
            nc.vector.tensor_tensor(
                out=hid[:].rearrange("p (c i) t -> p c t i", i=4),
                in0=term[:].rearrange("p t (c i) -> p c t i", i=4),
                in1=lw[c][:].rearrange("p t (c i) -> p c t i", i=4),
                op=ALU.add,
            )
            codes = sb("codes%d" % c, [P, n], U32)
            plane = sb("plane%d" % c, [P, n], U8)
            nc.vector.quantize_mx(out=codes[:].bitcast(FP8X4), scales=plane[:], in_=hid[:].rearrange("p r t -> p (r t)"))
            result = sb("result%d" % c, [P, 2, n], F32)
            for b in range(2):
                acc = psum.tile([P, n], F32, name="out%d_%d" % (c, b), tag="bank%d" % (2 * c + b))
                for n0, nn in ((0, 256), (256, 128)) if n == 384 else ((0, n),):
                    nc.tensor.matmul_mx(
                        out=acc[:, n0 : n0 + nn],
                        lhsT=w3w[:, 2 * P * b : 2 * P * (b + 1)].bitcast(FP4X4),
                        lhsT_scale=w3s[:, P * b : P * (b + 1)],
                        rhs=codes[:, n0 : n0 + nn].bitcast(FP8X4),
                        rhs_scale=plane[:, n0 : n0 + nn],
                        start=True,
                        stop=True,
                    )
                if c == 2 and b == 1:
                    nc.vector.tensor_copy(out=result[:, b, :], in_=acc[:])
                else:
                    nc.scalar.copy(out=result[:, b, :], in_=acc[:])
            nc.sync.dma_start(out=out_v[:, :, r0 : r0 + n], in_=result[:])

        gather_a(0)
        absolute(0)
        gather_b(0)
        gather_a(1)
        weights(0)
        gather_b(1)
        weights(1)
        absolute(1)
        weigh(0)
        gather_a(2)
        gather_b_plain(2)
        finish(0)
        weigh(1)
        add_logs(2)
        weights(2)
        finish(1)
        weigh(2)
        finish(2)
